import numpy as np
import ml_dtypes


def mxq(x, axis, fmt="e4m3"):
    dtype, down = {"e4m3": (ml_dtypes.float8_e4m3fn, 7), "e5m2": (ml_dtypes.float8_e5m2, 14)}[fmt]
    v = np.moveaxis(np.asarray(x, np.float32).astype(ml_dtypes.bfloat16).astype(np.float64), axis, -1)
    blocks = v.reshape(v.shape[:-1] + (-1, 32))
    amax = np.abs(blocks).max(-1, keepdims=True)
    byte = np.maximum(np.where(amax > 0, np.frexp(amax)[1] - 1 + 127, 0) - down, 1)
    scale = np.exp2(byte - 127.0)
    codes = (blocks / scale).astype(np.float32).astype(dtype).astype(np.float64)
    return np.moveaxis((codes * scale).reshape(v.shape), -1, axis)


WIDE = False


def mx_kscale(k):
    if not WIDE:
        return np.ones(k)
    levels = np.array([10, -10, 5, -5, 0])
    if k % 512:
        return np.exp2(np.random.permutation(np.resize(levels, k // 32))).repeat(32)
    a = np.empty((k // 512, 16))
    for p in range(k // 512):
        a[p, :8] = np.random.permutation(np.resize(levels, 8))
        for g in range(8):
            far = levels[np.abs(levels - a[p, g]) >= 10]
            a[p, g + 8] = far[np.random.randint(len(far))]
    return np.exp2(a.ravel()).repeat(32)


def f64(x):
    return np.asarray(x).astype(np.float64)


def striped(idx):
    return np.tile(idx.reshape(-1, 16).T, (8, 1)).astype(np.uint16)


def unstriped(offs):
    return offs[:16].T.reshape(-1).astype(np.int64)


E2M1 = np.array([0.0, 0.5, 1.0, 1.5, 2.0, 3.0, 4.0, 6.0, -0.0, -0.5, -1.0, -1.5, -2.0, -3.0, -4.0, -6.0])


def pack_weight(w, fmt):
    k, n = w.shape
    w = f64(np.asarray(w, np.float32).astype(ml_dtypes.bfloat16)).reshape(k // 32, 32, n)
    amax = np.abs(w).max(1)
    if fmt == "e4m3":
        byte = np.frexp(amax)[1] - 1 + 127 - 7
    else:
        mant, ex = np.frexp(amax / 6.0)
        byte = np.where(mant > 0.5, ex, ex - 1) + 127
    byte = np.clip(np.where(amax > 0, byte, 1), 1, 254)
    scaled = (w * np.exp2(127.0 - byte)[:, None, :]).reshape(k, n).astype(np.float32)
    by_word = np.ascontiguousarray(scaled.reshape(k // 512, 128, 4, n).transpose(0, 1, 3, 2))
    if fmt == "e4m3":
        words = by_word.astype(ml_dtypes.float8_e4m3fn).view(np.uint8)
    else:
        c = by_word.astype(ml_dtypes.float4_e2m1fn).view(np.uint8) & 0xF
        words = (c[..., 0::2] | (c[..., 1::2] << 4)).reshape(k // 512, 128, 2 * n)
    return np.ascontiguousarray(words), np.ascontiguousarray(byte.astype(np.uint8).reshape(k // 512, 16, n))


def unpack_weight(words, scales, fmt):
    g, _, n = scales.shape
    words = np.ascontiguousarray(words).reshape(g, 128, n, -1)
    if fmt == "e4m3":
        vals = words.view(ml_dtypes.float8_e4m3fn).astype(np.float64)
    else:
        nib = np.empty((g, 128, n, 4), np.uint8)
        nib[..., 0::2] = words & 0xF
        nib[..., 1::2] = words >> 4
        vals = E2M1[nib]
    vals = vals * np.repeat(np.exp2(scales.astype(np.float64) - 127.0), 8, axis=1)[..., None]
    return vals.transpose(0, 1, 3, 2).reshape(g * 512, n)


def gelu(v):
    return 0.5 * v * (1.0 + np.tanh(np.sqrt(2.0 / np.pi) * (v + 0.044715 * v**3)))


def striped8(idx):
    return np.concatenate([v.reshape(-1, 16).T for v in idx]).astype(np.uint16)


def unstriped8(offs):
    return np.stack([offs[16 * g:16 * g + 16].T.reshape(-1) for g in range(8)]).astype(np.int64)


def put_heads(h, wgs, idx8, t2):
    r = np.arange(h.shape[0])
    page = np.zeros((h.shape[0], t2))
    page[r[:, None], idx8[r % 512 // 64]] = wgs[r // 4 % 128] * h
    return page


K, T, S, H, T2, P, N = 1536, 2048, 512, 1024, 1024, 512, 768

def setup_inputs():
    n = np.random.standard_normal
    s = mx_kscale(K)[:, None]
    u = mx_kscale(H)[:, None]
    tab_words, tab_scales = pack_weight(n((K, T)) * s, "e4m3")
    w2_words, w2_scales = pack_weight(n((H, N)) / np.sqrt(H) / u, "e2m1")
    slots = np.stack([np.random.permutation(T2)[:S] for _ in range(8)])
    return {
        "tab_words": tab_words, "tab_scales": tab_scales,
        "offs": striped(np.random.permutation(T)[:S]),
        "offs2": striped8(slots),
        "offs3": striped(np.random.permutation(T2)[:P]),
        "w1": (1.2 * n((K, H)) / np.sqrt(K) / s).astype(np.float32),
        "b1": (0.5 * n(H)).astype(np.float32),
        "gm": (np.exp(0.5 * n((H, S))) * u).astype(np.float32),
        "wgs": np.repeat(np.random.uniform(0.5, 2.0, (8, S)), 16, axis=0).astype(np.float32),
        "bed": (0.7 * n((H, P)) * u).astype(np.float32),
        "w2_words": w2_words, "w2_scales": w2_scales,
        "gv": n((N, P)).astype(np.float32),
        "w3": (n((H, N)) / np.sqrt(H) / u).astype(np.float32),
    }

def reference(tab_words, tab_scales, offs, offs2, offs3, w1, b1, gm, wgs, bed,
              w2_words, w2_scales, gv, w3):
    v = unpack_weight(tab_words, tab_scales, "e4m3")[:, unstriped(offs)]
    q1 = mxq(f64(w1), 0, "e4m3")
    h = np.tanh((q1.T @ v) + f64(b1)[:, None]) * f64(gm)
    page = put_heads(h, f64(wgs), unstriped8(offs2), T2)
    x = page[:, unstriped(offs3)]
    z = mxq(x + f64(bed), 0, "e4m3")
    w2 = unpack_weight(w2_words, w2_scales, "e2m1")
    q3 = mxq(f64(w3), 0, "e4m3")
    y1 = w2.T @ z
    y2 = q3.T @ z
    return f64(gv) * y1 + np.abs(y2)

@@ -1,0 +1,297 @@
+from contextlib import ExitStack
+
+import concourse.mybir as mybir
+
+K, T, S, H, T2, M, N = 1536, 2048, 512, 1024, 1024, 512, 768
+FLOPS = 2 * (K * H * S + 2 * H * N * M)
+
+F32 = mybir.dt.float32
+BF16 = mybir.dt.bfloat16
+I32 = mybir.dt.int32
+U32 = mybir.dt.uint32
+U16 = mybir.dt.uint16
+U8 = mybir.dt.uint8
+FP8X4 = mybir.dt.float8_e4m3fn_x4
+FP4X4 = mybir.dt.float4_e2m1fn_x4
+MULT = mybir.AluOpType.mult
+ADD = mybir.AluOpType.add
+TANH = mybir.ActivationFunctionType.Tanh
+ABS = mybir.ActivationFunctionType.Abs
+
+P = 128
+PACK = 4
+KP = P * PACK
+K_PASSES = K // KP
+H_PASSES = H // KP
+SLICES = H_PASSES * PACK
+N_TILES = N // P
+PAGES = 3
+BANKS = 8
+
+
+def tile_list_beam_slot_features_kernel(
+    tc, tab_words, tab_scales, offs, offs2, offs3, w1, b1, gm, wgs, bed, w2_words, w2_scales, gv, w3, out
+):
+    nc = tc.nc
+    with ExitStack() as ctx:
+        lists = ctx.enter_context(tc.tile_pool(name="lists", bufs=1))
+        keep = ctx.enter_context(tc.tile_pool(name="keep", bufs=1))
+        psum = ctx.enter_context(tc.psum_pool(name="psum", bufs=1))
+
+        pick = lists.tile([P, S // 16], U16, name="pick")
+        put = lists.tile([P, S // 16], U16, name="put")
+        fetch = lists.tile([P, M // 16], U16, name="fetch")
+
+        def bank(i, name):
+            return psum.tile([P, 512], F32, name=name, tag="bank%d" % i)
+
+        def staged(name):
+            return keep.tile([P, KP * PACK], BF16, name=name, tag="staged", bufs=4, align_bytes=64)
+
+        tab_plane = keep.tile([P, T], U8, name="tab_plane", align_bytes=64)
+        nc.vector.memset(tab_plane[:].bitcast(I32), 0)
+        for q in range(4):
+            nc.scalar.dma_start(
+                out=tab_plane[32 * q : 32 * q + 4 * K_PASSES, :].bitcast(I32),
+                in_=tab_scales[:, 4 * q : 4 * q + 4, :].bitcast(I32),
+            )
+        w2_plane = keep.tile([P, H_PASSES * N], U8, name="w2_plane", align_bytes=64)
+        nc.vector.memset(w2_plane[:].bitcast(I32), 0)
+
+        pages = [keep.tile([P, T2], F32, name="page%d" % i) for i in range(PAGES)]
+        for page in pages:
+            nc.vector.memset(page[:], 0.0)
+
+        w1_raw = {}
+
+        def load_w1(b, a):
+            w1_raw[b, a] = keep.tile([P, PACK, KP], F32, name="w1_raw%d%d" % (b, a), tag="w1_raw", bufs=K_PASSES)
+            nc.sync.dma_start(
+                out=w1_raw[b, a][:],
+                in_=w1[a * KP : (a + 1) * KP, b * KP : (b + 1) * KP].rearrange("(p j) c -> p j c", j=PACK),
+            )
+
+        gain = {}
+        echo = {}
+        gm_rows = gm.rearrange("(b p i) j -> b i p j", p=P, i=PACK)
+        bed_rows = bed.rearrange("(b p i) m -> b i p m", p=P, i=PACK)
+
+        def load_gm(s):
+            last = s == SLICES - 1
+            gain[s] = keep.tile(
+                [P, S], F32, name="gain%d" % s, tag="last_gain" if last else "gain",
+                bufs=1 if last else SLICES - 1, align_bytes=64,
+            )
+            nc.sync.dma_start(out=gain[s][:], in_=gm_rows[s // PACK, s % PACK])
+
+        def load_bed(s):
+            echo[s] = keep.tile([P, M], F32, name="echo%d" % s)
+            nc.sync.dma_start(out=echo[s][:], in_=bed_rows[s // PACK, s % PACK])
+
+        w3_raw = {}
+
+        def load_w3(b):
+            w3_raw[b] = keep.tile([P, PACK, N], F32, name="w3_raw%d" % b)
+            nc.sync.dma_start(out=w3_raw[b][:], in_=w3[b * KP : (b + 1) * KP, :].rearrange("(p j) c -> p j c", j=PACK))
+
+        w1_codes = {}
+        w1_plane = {}
+
+        def quantise_w1(b, a):
+            rounded = staged("w1_bf%d%d" % (b, a))
+            nc.scalar.copy(
+                out=rounded[:].rearrange("p (i m j) -> p m j i", i=PACK, j=PACK),
+                in_=w1_raw[b, a][:].rearrange("p j (m i) -> p m j i", i=PACK),
+            )
+            w1_codes[b, a] = keep.tile([P, KP], U32, name="w1_codes%d%d" % (b, a), align_bytes=64)
+            w1_plane[b, a] = keep.tile([P, KP], U8, name="w1_plane%d%d" % (b, a), align_bytes=64)
+            nc.vector.quantize_mx(out=w1_codes[b, a][:].bitcast(FP8X4), scales=w1_plane[b, a][:], in_=rounded[:])
+
+        squashed = {}
+
+        def first_product(s):
+            b, i = divmod(s, PACK)
+            acc = bank(s, "h_acc%d" % s)
+            cols = slice(i * P, (i + 1) * P)
+            for a in range(K_PASSES):
+                nc.tensor.matmul_mx(
+                    out=acc[:],
+                    lhsT=w1_codes[b, a][:, cols].bitcast(FP8X4),
+                    lhsT_scale=w1_plane[b, a][:, cols],
+                    rhs=picked_words[a][:].bitcast(FP8X4),
+                    rhs_scale=picked_plane[4 * a : P, :],
+                    start=(a == 0),
+                    stop=(a == K_PASSES - 1),
+                )
+            squashed[s] = keep.tile([P, S], F32, name="squashed%d" % s, tag="squashed", bufs=SLICES)
+            nc.scalar.activation(out=squashed[s][:], in_=acc[:], func=TANH, bias=bias[:, s : s + 1])
+
+        def scale_gain(s):
+            nc.vector.tensor_tensor(gain[s][:], gain[s][:], slot_weight[:], MULT)
+
+        def scatter(s):
+            nc.vector.tensor_tensor(pages[s % PAGES][:].indirect(put[:]), squashed[s][:], gain[s][:], MULT)
+
+        cells = {}
+
+        def gather(s):
+            b, i = divmod(s, PACK)
+            if i == 0:
+                cells[b] = keep.tile([P, PACK, M], F32, name="cells%d" % b, tag="cells")
+            nc.vector.tensor_tensor(cells[b][:, i, :], pages[s % PAGES][:].indirect(fetch[:]), echo[s][:], ADD)
+
+        def interleave(copy, rounded, raw):
+            copy(
+                out=rounded.rearrange("p (c i j) -> p c j i", i=4, j=PACK),
+                in_=raw.rearrange("p j (c i) -> p c j i", i=4),
+            )
+
+        w3_codes = [keep.tile([P, N], U32, name="w3_codes%d" % b, align_bytes=64) for b in range(H_PASSES)]
+        w3_plane = [keep.tile([P, N], U8, name="w3_plane%d" % b, align_bytes=64) for b in range(H_PASSES)]
+
+        def quantise_w3(b):
+            for c0, c1 in ((0, 512), (512, N)):
+                rounded = staged("w3_bf%d_%d" % (b, c0))
+                width = (c1 - c0) * PACK
+                interleave(nc.scalar.copy, rounded[:, :width], w3_raw[b][:, :, c0:c1])
+                nc.vector.quantize_mx(
+                    out=w3_codes[b][:, c0:c1].bitcast(FP8X4), scales=w3_plane[b][:, c0:c1], in_=rounded[:, :width]
+                )
+
+        z_codes = {}
+        z_plane = {}
+        sums = {}
+
+        def second_pass(n, b):
+            cols = slice(n * P, (n + 1) * P)
+            if b == 0:
+                sums[n] = (bank((2 * n) % BANKS, "y1_%d" % n), bank((2 * n + 1) % BANKS, "y2_%d" % n))
+            y1, y2 = sums[n]
+            nc.tensor.matmul_mx(
+                out=y2[:], lhsT=w3_codes[b][:, cols].bitcast(FP8X4), lhsT_scale=w3_plane[b][:, cols],
+                rhs=z_codes[b][:].bitcast(FP8X4), rhs_scale=z_plane[b][:], start=(b == 0), stop=(b == H_PASSES - 1),
+            )
+            nc.tensor.matmul_mx(
+                out=y1[:], lhsT=w2_codes[:, b, 2 * n * P : 2 * (n + 1) * P].bitcast(FP4X4),
+                lhsT_scale=w2_plane[:, b * N + n * P : b * N + (n + 1) * P],
+                rhs=z_codes[b][:].bitcast(FP8X4), rhs_scale=z_plane[b][:], start=(b == 0), stop=(b == H_PASSES - 1),
+            )
+
+        gated = {}
+        size = {}
+
+        def leave_banks(n):
+            y1, y2 = sums[n]
+            size[n] = keep.tile([P, M], F32, name="size%d" % n, tag="squashed", bufs=SLICES)
+            nc.scalar.activation(out=size[n][:], in_=y2[:], func=ABS)
+            gated[n] = keep.tile([P, M], F32, name="gated%d" % n, tag="gain", bufs=SLICES - 1, align_bytes=64)
+            nc.vector.tensor_tensor(gated[n][:], y1[:], gate[n // 3][:, n % 3, :], MULT)
+
+        def finish(n):
+            nc.vector.tensor_tensor(gated[n][:], gated[n][:], size[n][:], ADD)
+            nc.sync.dma_start(out=out[n * P : (n + 1) * P, :], in_=gated[n][:])
+
+        nc.sync.dma_start(pick[:], offs)
+        nc.sync.dma_start(put[:], offs2)
+        nc.sync.dma_start(fetch[:], offs3)
+        bias = keep.tile([P, SLICES], F32, name="bias")
+        nc.sync.dma_start(out=bias[:].rearrange("p (b i) -> p b i", i=PACK), in_=b1.rearrange("(b p i) -> p b i", p=P, i=PACK))
+        for a in range(K_PASSES):
+            load_w1(0, a)
+        for a in range(K_PASSES):
+            quantise_w1(0, a)
+        picked_plane = keep.tile([P, S], U8, name="picked_plane", align_bytes=64)
+        nc.vector.tensor_copy(picked_plane[:], tab_plane[:].indirect(pick[:]))
+        picked_words = []
+        for a in range(K_PASSES):
+            table = keep.tile([P, T], U32, name="table%d" % a, align_bytes=64)
+            nc.sync.dma_start(out=table[:].bitcast(I32), in_=tab_words[a].rearrange("p t i -> p (t i)").bitcast(I32))
+            words = keep.tile([P, S], U32, name="picked_words%d" % a, align_bytes=64)
+            nc.vector.tensor_copy(words[:], table[:].indirect(pick[:]))
+            picked_words.append(words)
+        slot_weight = keep.tile([P, S], F32, name="slot_weight")
+        nc.sync.dma_start(out=slot_weight[:], in_=wgs)
+        load_gm(0)
+        scale_gain(0)
+        for s in range(PACK):
+            first_product(s)
+        load_gm(1)
+        load_bed(0)
+        load_w1(1, 0)
+        load_gm(2)
+        load_w1(1, 1)
+        load_bed(1)
+        load_w1(1, 2)
+        load_w3(0)
+        load_bed(2)
+        load_gm(3)
+        load_w3(1)
+        load_bed(3)
+        load_gm(4)
+        w2_codes = keep.tile([P, H_PASSES, 2 * N], U8, name="w2_codes", align_bytes=64)
+        nc.sync.dma_start(out=w2_codes[:].bitcast(I32), in_=w2_words.bitcast(I32).rearrange("b p c -> p b c"))
+        for q in range(4):
+            nc.sync.dma_start(
+                out=w2_plane[32 * q : 32 * q + 4, :].bitcast(I32).rearrange("r (b c) -> r b c", b=H_PASSES),
+                in_=w2_scales[:, 4 * q : 4 * q + 4, :].bitcast(I32).rearrange("b r c -> r b c"),
+            )
+        gate = []
+        for half in range(2):
+            rows = keep.tile([P, 3, M], F32, name="gate%d" % half)
+            nc.sync.dma_start(out=rows[:], in_=gv[half * 3 * P : (half + 1) * 3 * P, :].rearrange("(n p) m -> p n m", p=P))
+            gate.append(rows)
+        for s in range(5, SLICES):
+            load_gm(s)
+            load_bed(s - 1)
+        load_bed(SLICES - 1)
+
+        scatter(0)
+        scale_gain(1)
+        gather(0)
+        scatter(1)
+        quantise_w1(1, 0)
+        scale_gain(2)
+        quantise_w1(1, 1)
+        gather(1)
+        scatter(2)
+        quantise_w1(1, 2)
+        for s in range(PACK, SLICES):
+            first_product(s)
+        scale_gain(3)
+        gather(2)
+        scatter(3)
+        quantise_w3(0)
+        scale_gain(4)
+        gather(3)
+        quantise_w3(1)
+        z0_rounded = staged("z_bf0")
+        interleave(nc.scalar.copy, z0_rounded[:], cells[0][:])
+        for s in range(PACK, SLICES - 1):
+            scatter(s)
+            scale_gain(s + 1)
+            gather(s)
+        scatter(SLICES - 1)
+        z_codes[0] = keep.tile([P, M], U32, name="z_codes0", tag="last_gain", bufs=1, align_bytes=64)
+        z_plane[0] = keep.tile([P, M], U8, name="z_plane0", align_bytes=64)
+        nc.vector.quantize_mx(out=z_codes[0][:].bitcast(FP8X4), scales=z_plane[0][:], in_=z0_rounded[:])
+        gather(SLICES - 1)
+        for n in range(BANKS // 2):
+            second_pass(n, 0)
+        z_codes[1] = keep.tile([P, M], U32, name="z_codes1", align_bytes=64)
+        z_plane[1] = keep.tile([P, M], U8, name="z_plane1", align_bytes=64)
+        half_m = M // 2
+        for copy, m0 in ((nc.vector.tensor_copy, 0), (nc.scalar.copy, half_m)):
+            rounded = staged("z_bf1_%d" % m0)
+            interleave(copy, rounded[:, : half_m * PACK], cells[1][:, :, m0 : m0 + half_m])
+            nc.vector.quantize_mx(
+                out=z_codes[1][:, m0 : m0 + half_m].bitcast(FP8X4), scales=z_plane[1][:, m0 : m0 + half_m],
+                in_=rounded[:, : half_m * PACK],
+            )
+        for n in range(N_TILES):
+            if n >= BANKS // 2:
+                second_pass(n, 0)
+            second_pass(n, 1)
+            leave_banks(n)
+            if n > 0:
+                finish(n - 1)
+        finish(N_TILES - 1)

@@ -72,21 +72,20 @@ def tile_list_beam_slot_features_kernel(
             )
 
         gain = {}
-        echo = {}
         gm_rows = gm.rearrange("(b p i) j -> b i p j", p=P, i=PACK)
         bed_rows = bed.rearrange("(b p i) m -> b i p m", p=P, i=PACK)
 
         def load_gm(s):
-            last = s == SLICES - 1
-            gain[s] = keep.tile(
-                [P, S], F32, name="gain%d" % s, tag="last_gain" if last else "gain",
-                bufs=1 if last else SLICES - 1, align_bytes=64,
-            )
+            gain[s] = keep.tile([P, S], F32, name="gain%d" % s, tag="gain", bufs=SLICES)
             nc.sync.dma_start(out=gain[s][:], in_=gm_rows[s // PACK, s % PACK])
 
+        strip = keep.tile([P, (SLICES + 2) * M], F32, name="strip")
+
+        def region(r):
+            return strip[:, r * M : (r + 1) * M]
+
         def load_bed(s):
-            echo[s] = keep.tile([P, M], F32, name="echo%d" % s)
-            nc.sync.dma_start(out=echo[s][:], in_=bed_rows[s // PACK, s % PACK])
+            nc.sync.dma_start(out=region(s + 2), in_=bed_rows[s // PACK, s % PACK])
 
         w3_raw = {}
 
@@ -123,22 +122,26 @@ def tile_list_beam_slot_features_kernel(
                     start=(a == 0),
                     stop=(a == K_PASSES - 1),
                 )
-            squashed[s] = keep.tile([P, S], F32, name="squashed%d" % s, tag="squashed", bufs=SLICES)
-            nc.scalar.activation(out=squashed[s][:], in_=acc[:], func=TANH, bias=bias[:, s : s + 1])
+            last = s == SLICES - 1
+            squashed[s] = keep.tile(
+                [P, S], F32, name="squashed%d" % s, tag="last_squashed" if last else "squashed",
+                bufs=1 if last else SLICES - 1, align_bytes=64,
+            )
+            target = region(1) if s == 1 else squashed[s][:]
+            nc.scalar.activation(out=target, in_=acc[:], func=TANH, bias=bias[:, s : s + 1])
 
-        def scale_gain(s):
-            nc.vector.tensor_tensor(gain[s][:], gain[s][:], slot_weight[:], MULT)
+        def weigh(s):
+            nc.gpsimd.tensor_tensor(region(s - 1), gain[s][:], slot_weight[:], MULT)
+            nc.gpsimd.tensor_tensor(squashed[s][:], squashed[s][:], region(s - 1), MULT)
 
         def scatter(s):
-            nc.vector.tensor_tensor(pages[s % PAGES][:].indirect(put[:]), squashed[s][:], gain[s][:], MULT)
-
-        cells = {}
+            nc.vector.tensor_copy(pages[s % PAGES][:].indirect(put[:]), squashed[s][:])
 
         def gather(s):
-            b, i = divmod(s, PACK)
-            if i == 0:
-                cells[b] = keep.tile([P, PACK, M], F32, name="cells%d" % b, tag="cells")
-            nc.vector.tensor_tensor(cells[b][:, i, :], pages[s % PAGES][:].indirect(fetch[:]), echo[s][:], ADD)
+            nc.vector.tensor_tensor(region(s), pages[s % PAGES][:].indirect(fetch[:]), region(s + 2), ADD)
+
+        def cells(b):
+            return strip[:, b * PACK * M : (b + 1) * PACK * M].rearrange("p (j m) -> p j m", j=PACK)
 
         def interleave(copy, rounded, raw):
             copy(
@@ -168,12 +171,13 @@ def tile_list_beam_slot_features_kernel(
                 sums[n] = (bank((2 * n) % BANKS, "y1_%d" % n), bank((2 * n + 1) % BANKS, "y2_%d" % n))
             y1, y2 = sums[n]
             nc.tensor.matmul_mx(
-                out=y2[:], lhsT=w3_codes[b][:, cols].bitcast(FP8X4), lhsT_scale=w3_plane[b][:, cols],
-                rhs=z_codes[b][:].bitcast(FP8X4), rhs_scale=z_plane[b][:], start=(b == 0), stop=(b == H_PASSES - 1),
-            )
-            nc.tensor.matmul_mx(
                 out=y1[:], lhsT=w2_codes[:, b, 2 * n * P : 2 * (n + 1) * P].bitcast(FP4X4),
                 lhsT_scale=w2_plane[:, b * N + n * P : b * N + (n + 1) * P],
+                rhs=z_codes[b][:].bitcast(FP8X4), rhs_scale=z_plane[b][:], start=(b == 0), stop=(b == H_PASSES - 1),
+            )
+
+            nc.tensor.matmul_mx(
+                out=y2[:], lhsT=w3_codes[b][:, cols].bitcast(FP8X4), lhsT_scale=w3_plane[b][:, cols],
                 rhs=z_codes[b][:].bitcast(FP8X4), rhs_scale=z_plane[b][:], start=(b == 0), stop=(b == H_PASSES - 1),
             )
 
@@ -182,9 +186,9 @@ def tile_list_beam_slot_features_kernel(
 
         def leave_banks(n):
             y1, y2 = sums[n]
-            size[n] = keep.tile([P, M], F32, name="size%d" % n, tag="squashed", bufs=SLICES)
+            size[n] = keep.tile([P, M], F32, name="size%d" % n, tag="squashed", bufs=SLICES - 1, align_bytes=64)
             nc.scalar.activation(out=size[n][:], in_=y2[:], func=ABS)
-            gated[n] = keep.tile([P, M], F32, name="gated%d" % n, tag="gain", bufs=SLICES - 1, align_bytes=64)
+            gated[n] = keep.tile([P, M], F32, name="gated%d" % n, tag="gain", bufs=SLICES)
             nc.vector.tensor_tensor(gated[n][:], y1[:], gate[n // 3][:, n % 3, :], MULT)
 
         def finish(n):
@@ -212,22 +216,26 @@ def tile_list_beam_slot_features_kernel(
         slot_weight = keep.tile([P, S], F32, name="slot_weight")
         nc.sync.dma_start(out=slot_weight[:], in_=wgs)
         load_gm(0)
-        scale_gain(0)
+        nc.vector.tensor_tensor(gain[0][:], gain[0][:], slot_weight[:], MULT)
+        load_gm(1)
+        nc.vector.tensor_tensor(region(0), gain[1][:], slot_weight[:], MULT)
         for s in range(PACK):
             first_product(s)
-        load_gm(1)
-        load_bed(0)
         load_w1(1, 0)
         load_gm(2)
         load_w1(1, 1)
-        load_bed(1)
+        load_bed(0)
         load_w1(1, 2)
-        load_w3(0)
-        load_bed(2)
         load_gm(3)
-        load_w3(1)
-        load_bed(3)
+        load_bed(1)
         load_gm(4)
+        load_bed(2)
+        load_w3(0)
+        load_gm(5)
+        load_bed(3)
+        load_w3(1)
+        load_gm(6)
+        load_bed(4)
         w2_codes = keep.tile([P, H_PASSES, 2 * N], U8, name="w2_codes", align_bytes=64)
         nc.sync.dma_start(out=w2_codes[:].bitcast(I32), in_=w2_words.bitcast(I32).rearrange("b p c -> p b c"))
         for q in range(4):
@@ -240,40 +248,33 @@ def tile_list_beam_slot_features_kernel(
             rows = keep.tile([P, 3, M], F32, name="gate%d" % half)
             nc.sync.dma_start(out=rows[:], in_=gv[half * 3 * P : (half + 1) * 3 * P, :].rearrange("(n p) m -> p n m", p=P))
             gate.append(rows)
+        load_gm(7)
         for s in range(5, SLICES):
-            load_gm(s)
-            load_bed(s - 1)
-        load_bed(SLICES - 1)
+            load_bed(s)
 
-        scatter(0)
-        scale_gain(1)
-        gather(0)
+        nc.vector.tensor_tensor(pages[0][:].indirect(put[:]), squashed[0][:], gain[0][:], MULT)
+        nc.vector.tensor_tensor(squashed[1][:], region(1), region(0), MULT)
         scatter(1)
-        quantise_w1(1, 0)
-        scale_gain(2)
-        quantise_w1(1, 1)
-        gather(1)
-        scatter(2)
-        quantise_w1(1, 2)
+        weigh(2)
+        gather(0)
+        for a in range(K_PASSES):
+            quantise_w1(1, a)
         for s in range(PACK, SLICES):
             first_product(s)
-        scale_gain(3)
-        gather(2)
-        scatter(3)
-        quantise_w3(0)
-        scale_gain(4)
-        gather(3)
-        quantise_w3(1)
-        z0_rounded = staged("z_bf0")
-        interleave(nc.scalar.copy, z0_rounded[:], cells[0][:])
-        for s in range(PACK, SLICES - 1):
+        for s in range(2, SLICES - 1):
             scatter(s)
-            scale_gain(s + 1)
-            gather(s)
+            weigh(s + 1)
+            gather(s - 1)
+            if s in (2, 3):
+                quantise_w3(s - 2)
+            if s == PACK:
+                z0_rounded = staged("z_bf0")
+                interleave(nc.scalar.copy, z0_rounded[:], cells(0))
         scatter(SLICES - 1)
-        z_codes[0] = keep.tile([P, M], U32, name="z_codes0", tag="last_gain", bufs=1, align_bytes=64)
+        z_codes[0] = keep.tile([P, M], U32, name="z_codes0", tag="last_squashed", bufs=1, align_bytes=64)
         z_plane[0] = keep.tile([P, M], U8, name="z_plane0", align_bytes=64)
         nc.vector.quantize_mx(out=z_codes[0][:].bitcast(FP8X4), scales=z_plane[0][:], in_=z0_rounded[:])
+        gather(SLICES - 2)
         gather(SLICES - 1)
         for n in range(BANKS // 2):
             second_pass(n, 0)
@@ -282,7 +283,7 @@ def tile_list_beam_slot_features_kernel(
         half_m = M // 2
         for copy, m0 in ((nc.vector.tensor_copy, 0), (nc.scalar.copy, half_m)):
             rounded = staged("z_bf1_%d" % m0)
-            interleave(copy, rounded[:, : half_m * PACK], cells[1][:, :, m0 : m0 + half_m])
+            interleave(copy, rounded[:, : half_m * PACK], cells(1)[:, :, m0 : m0 + half_m])
             nc.vector.quantize_mx(
                 out=z_codes[1][:, m0 : m0 + half_m].bitcast(FP8X4), scales=z_plane[1][:, m0 : m0 + half_m],
                 in_=rounded[:, : half_m * PACK],

@@ -1,6 +1,7 @@
 from contextlib import ExitStack
 
 import concourse.mybir as mybir
+from concourse.masks import make_identity
 
 K, T, S, H, T2, M, N = 1536, 2048, 512, 1024, 1024, 512, 768
 FLOPS = 2 * (K * H * S + 2 * H * N * M)
@@ -25,7 +26,8 @@ K_PASSES = K // KP
 H_PASSES = H // KP
 SLICES = H_PASSES * PACK
 N_TILES = N // P
-PAGES = 3
+PAGES = 2
+FUSED = SLICES - 2
 BANKS = 8
 
 
@@ -46,15 +48,17 @@ def tile_list_beam_slot_features_kernel(
             return psum.tile([P, 512], F32, name=name, tag="bank%d" % i)
 
         def staged(name):
-            return keep.tile([P, KP * PACK], BF16, name=name, tag="staged", bufs=4, align_bytes=64)
+            return keep.tile([P, KP * PACK], BF16, name=name, tag="staged", bufs=3, align_bytes=64)
 
         tab_plane = keep.tile([P, T], U8, name="tab_plane", align_bytes=64)
-        nc.vector.memset(tab_plane[:].bitcast(I32), 0)
+        nc.gpsimd.memset(tab_plane[:].bitcast(I32), 0)
         for q in range(4):
-            nc.scalar.dma_start(
+            nc.gpsimd.dma_start(
                 out=tab_plane[32 * q : 32 * q + 4 * K_PASSES, :].bitcast(I32),
                 in_=tab_scales[:, 4 * q : 4 * q + 4, :].bitcast(I32),
             )
+        identity = keep.tile([P, P], F32, name="identity")
+        make_identity(nc, identity[:])
         w2_plane = keep.tile([P, H_PASSES * N], U8, name="w2_plane", align_bytes=64)
         nc.vector.memset(w2_plane[:].bitcast(I32), 0)
 
@@ -72,6 +76,7 @@ def tile_list_beam_slot_features_kernel(
             )
 
         gain = {}
+        echo = {}
         gm_rows = gm.rearrange("(b p i) j -> b i p j", p=P, i=PACK)
         bed_rows = bed.rearrange("(b p i) m -> b i p m", p=P, i=PACK)
 
@@ -79,13 +84,9 @@ def tile_list_beam_slot_features_kernel(
             gain[s] = keep.tile([P, S], F32, name="gain%d" % s, tag="gain", bufs=SLICES)
             nc.sync.dma_start(out=gain[s][:], in_=gm_rows[s // PACK, s % PACK])
 
-        strip = keep.tile([P, (SLICES + 2) * M], F32, name="strip")
-
-        def region(r):
-            return strip[:, r * M : (r + 1) * M]
-
         def load_bed(s):
-            nc.sync.dma_start(out=region(s + 2), in_=bed_rows[s // PACK, s % PACK])
+            echo[s] = keep.tile([P, M], F32, name="echo%d" % s)
+            nc.sync.dma_start(out=echo[s][:], in_=bed_rows[s // PACK, s % PACK])
 
         w3_raw = {}
 
@@ -97,8 +98,12 @@ def tile_list_beam_slot_features_kernel(
         w1_plane = {}
 
         def quantise_w1(b, a):
-            rounded = staged("w1_bf%d%d" % (b, a))
-            nc.scalar.copy(
+            if (b, a) == (H_PASSES - 1, K_PASSES - 1):
+                rounded = keep.tile([P, KP * PACK], BF16, name="w1_bf_last", tag="w1_last", align_bytes=64)
+            else:
+                rounded = staged("w1_bf%d%d" % (b, a))
+            copy = nc.vector.tensor_copy if (b, a) == (0, K_PASSES - 1) else nc.scalar.copy
+            copy(
                 out=rounded[:].rearrange("p (i m j) -> p m j i", i=PACK, j=PACK),
                 in_=w1_raw[b, a][:].rearrange("p j (m i) -> p m j i", i=PACK),
             )
@@ -127,21 +132,47 @@ def tile_list_beam_slot_features_kernel(
                 [P, S], F32, name="squashed%d" % s, tag="last_squashed" if last else "squashed",
                 bufs=1 if last else SLICES - 1, align_bytes=64,
             )
-            target = region(1) if s == 1 else squashed[s][:]
-            nc.scalar.activation(out=target, in_=acc[:], func=TANH, bias=bias[:, s : s + 1])
+            nc.scalar.activation(out=squashed[s][:], in_=acc[:], func=TANH, bias=bias[:, s : s + 1])
+
+        weight = {}
 
         def weigh(s):
-            nc.gpsimd.tensor_tensor(region(s - 1), gain[s][:], slot_weight[:], MULT)
-            nc.gpsimd.tensor_tensor(squashed[s][:], squashed[s][:], region(s - 1), MULT)
+            weight[s] = keep.tile([P, S], F32, name="weight%d" % s, tag="weight", bufs=2)
+            nc.vector.tensor_tensor(weight[s][:], gain[s][:], slot_weight[:], MULT)
 
         def scatter(s):
-            nc.vector.tensor_copy(pages[s % PAGES][:].indirect(put[:]), squashed[s][:])
+            nc.vector.tensor_tensor(pages[s % PAGES][:].indirect(put[:]), squashed[s][:], weight[s][:], MULT)
+
+        turned = {}
 
         def gather(s):
-            nc.vector.tensor_tensor(region(s), pages[s % PAGES][:].indirect(fetch[:]), region(s + 2), ADD)
+            if s == 1:
+                cells = keep.tile([P, M], F32, name="cells1", tag="w1_last", align_bytes=64)
+            elif s == FUSED - 1:
+                cells = keep.tile([P, M], F32, name="cells5", tag="w3_last", align_bytes=64)
+            else:
+                cells = keep.tile([P, M], F32, name="cells%d" % s, tag="gain", bufs=SLICES)
+            nc.vector.tensor_copy(cells[:], pages[s % PAGES][:].indirect(fetch[:]))
+            pair, e = divmod(s, 2)
+            if e == 0:
+                turned[pair] = [bank(h, "turned%d_%d" % (pair, h)) for h in range(2)]
+            for mt in range(M // P):
+                spot = turned[pair][mt // 2][:, (mt % 2 * 2 + e) * P : (mt % 2 * 2 + e + 1) * P]
+                cols = slice(mt * P, (mt + 1) * P)
+                nc.tensor.matmul(spot, echo[s][:, cols], identity[:], start=True, stop=False, is_transpose=True)
+                nc.tensor.matmul(spot, cells[:, cols], identity[:], start=False, stop=True, is_transpose=True)
 
-        def cells(b):
-            return strip[:, b * PACK * M : (b + 1) * PACK * M].rearrange("p (j m) -> p j m", j=PACK)
+        def round_pair(pair, spot_of):
+            for h in range(2):
+                pairs = keep.tile([P, 2 * P * 2], BF16, name="pairs%d_%d" % (pair, h), tag="pairs", bufs=4)
+                nc.scalar.copy(
+                    out=pairs[:].rearrange("q (mt p e) -> q mt p e", mt=2, e=2),
+                    in_=turned[pair][h][:].rearrange("q (mt e p) -> q mt p e", mt=2, e=2),
+                )
+                for mt in range(2):
+                    nc.tensor.transpose(
+                        spot_of(2 * h + mt), pairs[:].bitcast(F32)[:, mt * P : (mt + 1) * P], identity[:]
+                    )
 
         def interleave(copy, rounded, raw):
             copy(
@@ -154,8 +185,11 @@ def tile_list_beam_slot_features_kernel(
 
         def quantise_w3(b):
             for c0, c1 in ((0, 512), (512, N)):
-                rounded = staged("w3_bf%d_%d" % (b, c0))
                 width = (c1 - c0) * PACK
+                if (b, c1) == (H_PASSES - 1, N):
+                    rounded = keep.tile([P, width], BF16, name="w3_bf_last", tag="w3_last", align_bytes=64)
+                else:
+                    rounded = staged("w3_bf%d_%d" % (b, c0))
                 interleave(nc.scalar.copy, rounded[:, :width], w3_raw[b][:, :, c0:c1])
                 nc.vector.quantize_mx(
                     out=w3_codes[b][:, c0:c1].bitcast(FP8X4), scales=w3_plane[b][:, c0:c1], in_=rounded[:, :width]
@@ -175,7 +209,6 @@ def tile_list_beam_slot_features_kernel(
                 lhsT_scale=w2_plane[:, b * N + n * P : b * N + (n + 1) * P],
                 rhs=z_codes[b][:].bitcast(FP8X4), rhs_scale=z_plane[b][:], start=(b == 0), stop=(b == H_PASSES - 1),
             )
-
             nc.tensor.matmul_mx(
                 out=y2[:], lhsT=w3_codes[b][:, cols].bitcast(FP8X4), lhsT_scale=w3_plane[b][:, cols],
                 rhs=z_codes[b][:].bitcast(FP8X4), rhs_scale=z_plane[b][:], start=(b == 0), stop=(b == H_PASSES - 1),
@@ -191,17 +224,17 @@ def tile_list_beam_slot_features_kernel(
             gated[n] = keep.tile([P, M], F32, name="gated%d" % n, tag="gain", bufs=SLICES)
             nc.vector.tensor_tensor(gated[n][:], y1[:], gate[n // 3][:, n % 3, :], MULT)
 
-        def finish(n):
-            nc.vector.tensor_tensor(gated[n][:], gated[n][:], size[n][:], ADD)
-            nc.sync.dma_start(out=out[n * P : (n + 1) * P, :], in_=gated[n][:])
+        def finish(n, m0, m1):
+            nc.vector.tensor_tensor(gated[n][:, m0:m1], gated[n][:, m0:m1], size[n][:, m0:m1], ADD)
+            nc.sync.dma_start(out=out[n * P : (n + 1) * P, m0:m1], in_=gated[n][:, m0:m1])
 
+        load_w1(0, 0)
         nc.sync.dma_start(pick[:], offs)
-        nc.sync.dma_start(put[:], offs2)
-        nc.sync.dma_start(fetch[:], offs3)
+        load_w1(0, 1)
+        load_w1(0, 2)
         bias = keep.tile([P, SLICES], F32, name="bias")
         nc.sync.dma_start(out=bias[:].rearrange("p (b i) -> p b i", i=PACK), in_=b1.rearrange("(b p i) -> p b i", p=P, i=PACK))
-        for a in range(K_PASSES):
-            load_w1(0, a)
+        nc.sync.dma_start(put[:], offs2)
         for a in range(K_PASSES):
             quantise_w1(0, a)
         picked_plane = keep.tile([P, S], U8, name="picked_plane", align_bytes=64)
@@ -216,26 +249,20 @@ def tile_list_beam_slot_features_kernel(
         slot_weight = keep.tile([P, S], F32, name="slot_weight")
         nc.sync.dma_start(out=slot_weight[:], in_=wgs)
         load_gm(0)
-        nc.vector.tensor_tensor(gain[0][:], gain[0][:], slot_weight[:], MULT)
         load_gm(1)
-        nc.vector.tensor_tensor(region(0), gain[1][:], slot_weight[:], MULT)
-        for s in range(PACK):
-            first_product(s)
-        load_w1(1, 0)
+        nc.sync.dma_start(fetch[:], offs3)
         load_gm(2)
-        load_w1(1, 1)
-        load_bed(0)
-        load_w1(1, 2)
         load_gm(3)
-        load_bed(1)
-        load_gm(4)
-        load_bed(2)
-        load_w3(0)
-        load_gm(5)
-        load_bed(3)
-        load_w3(1)
-        load_gm(6)
+        for a in range(K_PASSES):
+            load_w1(1, a)
+        for s in range(PACK, SLICES):
+            load_gm(s)
+        for b in range(H_PASSES):
+            load_bed(2 * b)
+            load_bed(2 * b + 1)
+            load_w3(b)
         load_bed(4)
+        load_bed(5)
         w2_codes = keep.tile([P, H_PASSES, 2 * N], U8, name="w2_codes", align_bytes=64)
         nc.sync.dma_start(out=w2_codes[:].bitcast(I32), in_=w2_words.bitcast(I32).rearrange("b p c -> p b c"))
         for q in range(4):
@@ -243,50 +270,76 @@ def tile_list_beam_slot_features_kernel(
                 out=w2_plane[32 * q : 32 * q + 4, :].bitcast(I32).rearrange("r (b c) -> r b c", b=H_PASSES),
                 in_=w2_scales[:, 4 * q : 4 * q + 4, :].bitcast(I32).rearrange("b r c -> r b c"),
             )
+        load_bed(6)
+        load_bed(7)
         gate = []
         for half in range(2):
             rows = keep.tile([P, 3, M], F32, name="gate%d" % half)
             nc.sync.dma_start(out=rows[:], in_=gv[half * 3 * P : (half + 1) * 3 * P, :].rearrange("(n p) m -> p n m", p=P))
             gate.append(rows)
-        load_gm(7)
-        for s in range(5, SLICES):
-            load_bed(s)
 
-        nc.vector.tensor_tensor(pages[0][:].indirect(put[:]), squashed[0][:], gain[0][:], MULT)
-        nc.vector.tensor_tensor(squashed[1][:], region(1), region(0), MULT)
-        scatter(1)
-        weigh(2)
-        gather(0)
-        for a in range(K_PASSES):
-            quantise_w1(1, a)
-        for s in range(PACK, SLICES):
+        half_m = M // 2
+        z_rounded = [keep.tile([P, M * PACK], BF16, name="z_bf%d" % b, align_bytes=64) for b in range(H_PASSES)]
+        z_words = [z_rounded[b][:].bitcast(F32).rearrange("p (m u) -> p m u", u=2) for b in range(H_PASSES)]
+        weigh(0)
+        for s in range(PACK):
             first_product(s)
-        for s in range(2, SLICES - 1):
+        for s in range(FUSED):
             scatter(s)
             weigh(s + 1)
-            gather(s - 1)
-            if s in (2, 3):
-                quantise_w3(s - 2)
-            if s == PACK:
-                z0_rounded = staged("z_bf0")
-                interleave(nc.scalar.copy, z0_rounded[:], cells(0))
-        scatter(SLICES - 1)
+            if s == 1:
+                for a in range(K_PASSES):
+                    quantise_w1(1, a)
+                for later in range(PACK, SLICES):
+                    first_product(later)
+            if s == FUSED - 1:
+                for b in range(H_PASSES):
+                    quantise_w3(b)
+            gather(s)
+            if s == 1:
+                back = [bank(2 + h, "back0_%d" % h) for h in range(2)]
+            if s in (1, 3):
+                u = s // 2
+                round_pair(u, lambda mt: back[mt // 2][:, u * half_m + mt % 2 * P : u * half_m + (mt % 2 + 1) * P])
+            if s == 3:
+                for h in range(2):
+                    nc.scalar.copy(
+                        out=z_words[0][:, h * half_m : (h + 1) * half_m, :],
+                        in_=back[h][:].rearrange("p (u m) -> p m u", u=2),
+                    )
+        back1 = bank(2, "back1")
+        round_pair(2, lambda mt: back1[:, mt * P : (mt + 1) * P])
+        nc.scalar.copy(out=z_words[1][:, :, 0], in_=back1[:])
+
+        last_cells = keep.tile([P, 2, M], F32, name="last_cells")
+        scatter(FUSED)
+        weigh(FUSED + 1)
+        nc.vector.tensor_tensor(last_cells[:, 0, :], pages[FUSED % PAGES][:].indirect(fetch[:]), echo[FUSED][:], ADD)
+        scatter(FUSED + 1)
         z_codes[0] = keep.tile([P, M], U32, name="z_codes0", tag="last_squashed", bufs=1, align_bytes=64)
         z_plane[0] = keep.tile([P, M], U8, name="z_plane0", align_bytes=64)
-        nc.vector.quantize_mx(out=z_codes[0][:].bitcast(FP8X4), scales=z_plane[0][:], in_=z0_rounded[:])
-        gather(SLICES - 2)
-        gather(SLICES - 1)
+        nc.vector.quantize_mx(out=z_codes[0][:].bitcast(FP8X4), scales=z_plane[0][:], in_=z_rounded[0][:])
+        for m0 in (0, half_m):
+            nc.vector.tensor_tensor(
+                last_cells[:, 1, m0 : m0 + half_m],
+                pages[(FUSED + 1) % PAGES][:].indirect(fetch[:, m0 // 16 : (m0 + half_m) // 16]),
+                echo[FUSED + 1][:, m0 : m0 + half_m],
+                ADD,
+            )
         for n in range(BANKS // 2):
             second_pass(n, 0)
         z_codes[1] = keep.tile([P, M], U32, name="z_codes1", align_bytes=64)
         z_plane[1] = keep.tile([P, M], U8, name="z_plane1", align_bytes=64)
-        half_m = M // 2
-        for copy, m0 in ((nc.vector.tensor_copy, 0), (nc.scalar.copy, half_m)):
-            rounded = staged("z_bf1_%d" % m0)
-            interleave(copy, rounded[:, : half_m * PACK], cells(1)[:, :, m0 : m0 + half_m])
+        upper = z_rounded[1][:].rearrange("p (c i j) -> p c j i", i=4, j=PACK)[:, :, 2:4, :]
+        for m0 in (0, half_m):
+            nc.vector.tensor_copy(
+                out=upper[:, m0 // 4 : (m0 + half_m) // 4],
+                in_=last_cells[:, :, m0 : m0 + half_m].rearrange("p e (c i) -> p c e i", i=4),
+            )
+        for m0 in (0, half_m):
             nc.vector.quantize_mx(
                 out=z_codes[1][:, m0 : m0 + half_m].bitcast(FP8X4), scales=z_plane[1][:, m0 : m0 + half_m],
-                in_=rounded[:, : half_m * PACK],
+                in_=z_rounded[1][:, m0 * PACK : (m0 + half_m) * PACK],
             )
         for n in range(N_TILES):
             if n >= BANKS // 2:
@@ -294,5 +347,6 @@ def tile_list_beam_slot_features_kernel(
             second_pass(n, 1)
             leave_banks(n)
             if n > 0:
-                finish(n - 1)
-        finish(N_TILES - 1)
+                finish(n - 1, 0, M)
+        finish(N_TILES - 1, 0, half_m)
+        finish(N_TILES - 1, half_m, M)

@@ -26,7 +26,8 @@ K_PASSES = K // KP
 H_PASSES = H // KP
 SLICES = H_PASSES * PACK
 N_TILES = N // P
-PAGES = 2
+PAGES = 3
+PAGE_OF = (0, 1, 2, 1, 0, 2, 1, 2)
 FUSED = SLICES - 2
 BANKS = 8
 
@@ -38,6 +39,7 @@ def tile_list_beam_slot_features_kernel(
     with ExitStack() as ctx:
         lists = ctx.enter_context(tc.tile_pool(name="lists", bufs=1))
         keep = ctx.enter_context(tc.tile_pool(name="keep", bufs=1))
+        relay = ctx.enter_context(tc.tile_pool(name="relay", bufs=1))
         psum = ctx.enter_context(tc.psum_pool(name="psum", bufs=1))
 
         pick = lists.tile([P, S // 16], U16, name="pick")
@@ -50,10 +52,13 @@ def tile_list_beam_slot_features_kernel(
         def staged(name):
             return keep.tile([P, KP * PACK], BF16, name=name, tag="staged", bufs=3, align_bytes=64)
 
+        def slot(tag, name, shape=(P, S), dtype=F32):
+            return keep.tile(list(shape), dtype, name=name, tag=tag, align_bytes=64)
+
         tab_plane = keep.tile([P, T], U8, name="tab_plane", align_bytes=64)
-        nc.gpsimd.memset(tab_plane[:].bitcast(I32), 0)
+        nc.vector.memset(tab_plane[:].bitcast(I32), 0)
         for q in range(4):
-            nc.gpsimd.dma_start(
+            nc.scalar.dma_start(
                 out=tab_plane[32 * q : 32 * q + 4 * K_PASSES, :].bitcast(I32),
                 in_=tab_scales[:, 4 * q : 4 * q + 4, :].bitcast(I32),
             )
@@ -81,7 +86,7 @@ def tile_list_beam_slot_features_kernel(
         bed_rows = bed.rearrange("(b p i) m -> b i p m", p=P, i=PACK)
 
         def load_gm(s):
-            gain[s] = keep.tile([P, S], F32, name="gain%d" % s, tag="gain", bufs=SLICES)
+            gain[s] = slot("gain%d" % s, "gain%d" % s)
             nc.sync.dma_start(out=gain[s][:], in_=gm_rows[s // PACK, s % PACK])
 
         def load_bed(s):
@@ -91,25 +96,38 @@ def tile_list_beam_slot_features_kernel(
         w3_raw = {}
 
         def load_w3(b):
-            w3_raw[b] = keep.tile([P, PACK, N], F32, name="w3_raw%d" % b)
+            w3_raw[b] = slot("w3_raw%d" % b, "w3_raw%d" % b, (P, PACK, N))
             nc.sync.dma_start(out=w3_raw[b][:], in_=w3[b * KP : (b + 1) * KP, :].rearrange("(p j) c -> p j c", j=PACK))
 
         w1_codes = {}
         w1_plane = {}
 
-        def quantise_w1(b, a):
-            if (b, a) == (H_PASSES - 1, K_PASSES - 1):
-                rounded = keep.tile([P, KP * PACK], BF16, name="w1_bf_last", tag="w1_last", align_bytes=64)
-            else:
-                rounded = staged("w1_bf%d%d" % (b, a))
-            copy = nc.vector.tensor_copy if (b, a) == (0, K_PASSES - 1) else nc.scalar.copy
+        def round_w1(copy, rounded, b, a):
             copy(
-                out=rounded[:].rearrange("p (i m j) -> p m j i", i=PACK, j=PACK),
+                out=rounded.rearrange("p (i m j) -> p m j i", i=PACK, j=PACK),
                 in_=w1_raw[b, a][:].rearrange("p j (m i) -> p m j i", i=PACK),
             )
-            w1_codes[b, a] = keep.tile([P, KP], U32, name="w1_codes%d%d" % (b, a), align_bytes=64)
-            w1_plane[b, a] = keep.tile([P, KP], U8, name="w1_plane%d%d" % (b, a), align_bytes=64)
-            nc.vector.quantize_mx(out=w1_codes[b, a][:].bitcast(FP8X4), scales=w1_plane[b, a][:], in_=rounded[:])
+
+        def quantise_w1(copy, b, a, codes_tag):
+            rounded = staged("w1_bf%d%d" % (b, a))
+            round_w1(copy, rounded[:], b, a)
+            codes = slot(codes_tag, "w1_codes%d%d" % (b, a), (P, KP), U32)
+            plane = keep.tile([P, KP], U8, name="w1_plane%d%d" % (b, a), align_bytes=64)
+            nc.vector.quantize_mx(out=codes[:].bitcast(FP8X4), scales=plane[:], in_=rounded[:])
+            w1_codes[b, a], w1_plane[b, a] = codes[:], plane[:]
+
+        def relayed(name, row, shape=(P, M), dtype=F32):
+            return relay.tile(list(shape), dtype, name=name, offset=row * M * 4, align_bytes=64)
+
+        def quantise_w1_tail():
+            rounded = relayed("w1_bf_tail", 0, (P, 2 * KP * PACK), BF16)
+            codes = keep.tile([P, 2 * KP], U32, name="w1_tail_codes", align_bytes=64)
+            plane = keep.tile([P, 2 * KP], U8, name="w1_tail_plane", align_bytes=64)
+            for a in (1, 2):
+                round_w1(nc.scalar.copy, rounded[:, (a - 1) * KP * PACK : a * KP * PACK], 1, a)
+                w1_codes[1, a] = codes[:, (a - 1) * KP : a * KP]
+                w1_plane[1, a] = plane[:, (a - 1) * KP : a * KP]
+            nc.vector.quantize_mx(out=codes[:].bitcast(FP8X4), scales=plane[:], in_=rounded[:])
 
         squashed = {}
 
@@ -127,32 +145,26 @@ def tile_list_beam_slot_features_kernel(
                     start=(a == 0),
                     stop=(a == K_PASSES - 1),
                 )
-            last = s == SLICES - 1
-            squashed[s] = keep.tile(
-                [P, S], F32, name="squashed%d" % s, tag="last_squashed" if last else "squashed",
-                bufs=1 if last else SLICES - 1, align_bytes=64,
-            )
+            squashed[s] = slot("squashed%d" % s, "squashed%d" % s)
             nc.scalar.activation(out=squashed[s][:], in_=acc[:], func=TANH, bias=bias[:, s : s + 1])
 
-        weight = {}
+        weighted = {}
 
         def weigh(s):
-            weight[s] = keep.tile([P, S], F32, name="weight%d" % s, tag="weight", bufs=2)
-            nc.vector.tensor_tensor(weight[s][:], gain[s][:], slot_weight[:], MULT)
+            factor = relayed("factor%d" % s, 0) if s >= PACK else slot("squashed0", "factor%d" % s)
+            nc.gpsimd.tensor_tensor(factor[:], gain[s][:], slot_weight[:], MULT)
+            weighted[s] = slot("gain%d" % (s % 2), "weighted%d" % s)
+            nc.gpsimd.tensor_tensor(weighted[s][:], squashed[s][:], factor[:], MULT)
 
         def scatter(s):
-            nc.vector.tensor_tensor(pages[s % PAGES][:].indirect(put[:]), squashed[s][:], weight[s][:], MULT)
+            nc.vector.tensor_copy(pages[PAGE_OF[s]][:].indirect(put[:]), weighted[s][:])
 
         turned = {}
 
-        def gather(s):
-            if s == 1:
-                cells = keep.tile([P, M], F32, name="cells1", tag="w1_last", align_bytes=64)
-            elif s == FUSED - 1:
-                cells = keep.tile([P, M], F32, name="cells5", tag="w3_last", align_bytes=64)
-            else:
-                cells = keep.tile([P, M], F32, name="cells%d" % s, tag="gain", bufs=SLICES)
-            nc.vector.tensor_copy(cells[:], pages[s % PAGES][:].indirect(fetch[:]))
+        def gather(s, cells):
+            nc.vector.tensor_copy(cells, pages[PAGE_OF[s]][:].indirect(fetch[:]))
+
+        def add_echo(s, cells):
             pair, e = divmod(s, 2)
             if e == 0:
                 turned[pair] = [bank(h, "turned%d_%d" % (pair, h)) for h in range(2)]
@@ -163,15 +175,16 @@ def tile_list_beam_slot_features_kernel(
                 nc.tensor.matmul(spot, cells[:, cols], identity[:], start=False, stop=True, is_transpose=True)
 
         def round_pair(pair, spot_of):
+            both = slot("w3_raw1" if pair == 1 else "pairs%d" % pair, "pairs%d" % pair, (P, 2 * M), BF16)
             for h in range(2):
-                pairs = keep.tile([P, 2 * P * 2], BF16, name="pairs%d_%d" % (pair, h), tag="pairs", bufs=4)
+                pairs = both[:, h * M : (h + 1) * M]
                 nc.scalar.copy(
-                    out=pairs[:].rearrange("q (mt p e) -> q mt p e", mt=2, e=2),
+                    out=pairs.rearrange("q (mt p e) -> q mt p e", mt=2, e=2),
                     in_=turned[pair][h][:].rearrange("q (mt e p) -> q mt p e", mt=2, e=2),
                 )
                 for mt in range(2):
                     nc.tensor.transpose(
-                        spot_of(2 * h + mt), pairs[:].bitcast(F32)[:, mt * P : (mt + 1) * P], identity[:]
+                        spot_of(2 * h + mt), pairs.bitcast(F32)[:, mt * P : (mt + 1) * P], identity[:]
                     )
 
         def interleave(copy, rounded, raw):
@@ -180,19 +193,28 @@ def tile_list_beam_slot_features_kernel(
                 in_=raw.rearrange("p j (c i) -> p c j i", i=4),
             )
 
-        w3_codes = [keep.tile([P, N], U32, name="w3_codes%d" % b, align_bytes=64) for b in range(H_PASSES)]
+        w3_codes = {}
         w3_plane = [keep.tile([P, N], U8, name="w3_plane%d" % b, align_bytes=64) for b in range(H_PASSES)]
 
-        def quantise_w3(b):
-            for c0, c1 in ((0, 512), (512, N)):
-                width = (c1 - c0) * PACK
-                if (b, c1) == (H_PASSES - 1, N):
-                    rounded = keep.tile([P, width], BF16, name="w3_bf_last", tag="w3_last", align_bytes=64)
+        w3_pieces = [(b, c0, c1) for b in range(H_PASSES) for c0, c1 in ((0, N - 512), (N - 512, N))]
+        w3_rounded = {}
+
+        def round_w3():
+            for b, c0, c1 in w3_pieces:
+                if (b, c0, c1) == w3_pieces[-1]:
+                    whole = keep.tile([P, KP * PACK], BF16, name="w3_bf_tail", align_bytes=64)
                 else:
-                    rounded = staged("w3_bf%d_%d" % (b, c0))
-                interleave(nc.scalar.copy, rounded[:, :width], w3_raw[b][:, :, c0:c1])
+                    whole = staged("w3_bf%d_%d" % (b, c0))
+                w3_rounded[b, c0] = whole[:, : (c1 - c0) * PACK]
+                interleave(nc.scalar.copy, w3_rounded[b, c0], w3_raw[b][:, :, c0:c1])
+
+        def quantise_w3():
+            codes = slot("squashed6", "w3_codes", (P, H_PASSES * N), U32)
+            for b in range(H_PASSES):
+                w3_codes[b] = codes[:, b * N : (b + 1) * N]
+            for b, c0, c1 in w3_pieces:
                 nc.vector.quantize_mx(
-                    out=w3_codes[b][:, c0:c1].bitcast(FP8X4), scales=w3_plane[b][:, c0:c1], in_=rounded[:, :width]
+                    out=w3_codes[b][:, c0:c1].bitcast(FP8X4), scales=w3_plane[b][:, c0:c1], in_=w3_rounded[b, c0]
                 )
 
         z_codes = {}
@@ -202,7 +224,7 @@ def tile_list_beam_slot_features_kernel(
         def second_pass(n, b):
             cols = slice(n * P, (n + 1) * P)
             if b == 0:
-                sums[n] = (bank((2 * n) % BANKS, "y1_%d" % n), bank((2 * n + 1) % BANKS, "y2_%d" % n))
+                sums[n] = (bank((2 * n + 4) % BANKS, "y1_%d" % n), bank((2 * n + 5) % BANKS, "y2_%d" % n))
             y1, y2 = sums[n]
             nc.tensor.matmul_mx(
                 out=y1[:], lhsT=w2_codes[:, b, 2 * n * P : 2 * (n + 1) * P].bitcast(FP4X4),
@@ -219,24 +241,24 @@ def tile_list_beam_slot_features_kernel(
 
         def leave_banks(n):
             y1, y2 = sums[n]
-            size[n] = keep.tile([P, M], F32, name="size%d" % n, tag="squashed", bufs=SLICES - 1, align_bytes=64)
+            size[n] = slot("squashed%d" % (0, 1, 3, 7, 4, 5)[n], "size%d" % n)
             nc.scalar.activation(out=size[n][:], in_=y2[:], func=ABS)
-            gated[n] = keep.tile([P, M], F32, name="gated%d" % n, tag="gain", bufs=SLICES)
+            gated[n] = slot("gain%d" % (n + 2), "gated%d" % n)
             nc.vector.tensor_tensor(gated[n][:], y1[:], gate[n // 3][:, n % 3, :], MULT)
 
         def finish(n, m0, m1):
             nc.vector.tensor_tensor(gated[n][:, m0:m1], gated[n][:, m0:m1], size[n][:, m0:m1], ADD)
             nc.sync.dma_start(out=out[n * P : (n + 1) * P, m0:m1], in_=gated[n][:, m0:m1])
 
-        load_w1(0, 0)
         nc.sync.dma_start(pick[:], offs)
-        load_w1(0, 1)
-        load_w1(0, 2)
+        nc.sync.dma_start(fetch[:], offs3)
         bias = keep.tile([P, SLICES], F32, name="bias")
         nc.sync.dma_start(out=bias[:].rearrange("p (b i) -> p b i", i=PACK), in_=b1.rearrange("(b p i) -> p b i", p=P, i=PACK))
         nc.sync.dma_start(put[:], offs2)
         for a in range(K_PASSES):
-            quantise_w1(0, a)
+            load_w1(0, a)
+        for a in range(K_PASSES):
+            quantise_w1(nc.scalar.copy, 0, a, "w1_codes0%d" % a)
         picked_plane = keep.tile([P, S], U8, name="picked_plane", align_bytes=64)
         nc.vector.tensor_copy(picked_plane[:], tab_plane[:].indirect(pick[:]))
         picked_words = []
@@ -250,7 +272,6 @@ def tile_list_beam_slot_features_kernel(
         nc.sync.dma_start(out=slot_weight[:], in_=wgs)
         load_gm(0)
         load_gm(1)
-        nc.sync.dma_start(fetch[:], offs3)
         load_gm(2)
         load_gm(3)
         for a in range(K_PASSES):
@@ -279,50 +300,77 @@ def tile_list_beam_slot_features_kernel(
             gate.append(rows)
 
         half_m = M // 2
-        z_rounded = [keep.tile([P, M * PACK], BF16, name="z_bf%d" % b, align_bytes=64) for b in range(H_PASSES)]
+        z_rounded = [
+            relayed("z_bf0", 4, (P, M * PACK), BF16),
+            keep.tile([P, M * PACK], BF16, name="z_bf1", align_bytes=64),
+        ]
         z_words = [z_rounded[b][:].bitcast(F32).rearrange("p (m u) -> p m u", u=2) for b in range(H_PASSES)]
-        weigh(0)
+        nc.vector.tensor_tensor(gain[0][:], gain[0][:], slot_weight[:], MULT)
+        factor1 = slot("factor1", "factor1")
+        nc.vector.tensor_tensor(factor1[:], gain[1][:], slot_weight[:], MULT)
         for s in range(PACK):
             first_product(s)
-        for s in range(FUSED):
-            scatter(s)
-            weigh(s + 1)
-            if s == 1:
-                for a in range(K_PASSES):
-                    quantise_w1(1, a)
-                for later in range(PACK, SLICES):
-                    first_product(later)
-            if s == FUSED - 1:
-                for b in range(H_PASSES):
-                    quantise_w3(b)
-            gather(s)
-            if s == 1:
-                back = [bank(2 + h, "back0_%d" % h) for h in range(2)]
-            if s in (1, 3):
-                u = s // 2
-                round_pair(u, lambda mt: back[mt // 2][:, u * half_m + mt % 2 * P : u * half_m + (mt % 2 + 1) * P])
-            if s == 3:
-                for h in range(2):
-                    nc.scalar.copy(
-                        out=z_words[0][:, h * half_m : (h + 1) * half_m, :],
-                        in_=back[h][:].rearrange("p (u m) -> p m u", u=2),
-                    )
+        nc.vector.tensor_tensor(pages[PAGE_OF[0]][:].indirect(put[:]), squashed[0][:], gain[0][:], MULT)
+        weighted[1] = slot("gain1", "weighted1")
+        nc.vector.tensor_tensor(weighted[1][:], squashed[1][:], factor1[:], MULT)
+        scatter(1)
+        weigh(2)
+        cells0 = slot("factor1", "cells0")
+        gather(0, cells0[:])
+        add_echo(0, cells0[:])
+        scatter(2)
+        weigh(3)
+        quantise_w1(nc.scalar.copy, 1, 0, "squashed2")
+        quantise_w1_tail()
+        for s in range(PACK, SLICES):
+            first_product(s)
+        cells1 = relayed("cells1", 1)
+        gather(1, cells1[:])
+        add_echo(1, cells1[:])
+        back = [bank(2 + h, "back0_%d" % h) for h in range(2)]
+        round_pair(0, lambda mt: back[mt // 2][:, mt % 2 * P : (mt % 2 + 1) * P])
+        cells2 = relayed("cells2", 2)
+        gather(2, cells2[:])
+        add_echo(2, cells2[:])
+        weigh(4)
+        scatter(3)
+        weigh(5)
+        scatter(4)
+        weigh(6)
+        cells3 = slot("squashed4", "cells3")
+        gather(3, cells3[:])
+        add_echo(3, cells3[:])
+        scatter(5)
+        weigh(7)
+        cells4 = slot("squashed5", "cells4")
+        gather(4, cells4[:])
+        round_w3()
+        round_pair(1, lambda mt: back[mt // 2][:, half_m + mt % 2 * P : half_m + (mt % 2 + 1) * P])
+        for h in range(2):
+            nc.scalar.copy(
+                out=z_words[0][:, h * half_m : (h + 1) * half_m, :],
+                in_=back[h][:].rearrange("p (u m) -> p m u", u=2),
+            )
+        add_echo(4, cells4[:])
+        scatter(6)
+        quantise_w3()
+        z_codes[0] = relayed("z_codes0", 0, (P, M), U32)
+        z_plane[0] = keep.tile([P, M], U8, name="z_plane0", align_bytes=64)
+        nc.vector.quantize_mx(out=z_codes[0][:].bitcast(FP8X4), scales=z_plane[0][:], in_=z_rounded[0][:])
+        cells5 = relayed("cells5", 4)
+        gather(5, cells5[:])
+        add_echo(5, cells5[:])
         back1 = bank(2, "back1")
         round_pair(2, lambda mt: back1[:, mt * P : (mt + 1) * P])
         nc.scalar.copy(out=z_words[1][:, :, 0], in_=back1[:])
 
-        last_cells = keep.tile([P, 2, M], F32, name="last_cells")
-        scatter(FUSED)
-        weigh(FUSED + 1)
-        nc.vector.tensor_tensor(last_cells[:, 0, :], pages[FUSED % PAGES][:].indirect(fetch[:]), echo[FUSED][:], ADD)
-        scatter(FUSED + 1)
-        z_codes[0] = keep.tile([P, M], U32, name="z_codes0", tag="last_squashed", bufs=1, align_bytes=64)
-        z_plane[0] = keep.tile([P, M], U8, name="z_plane0", align_bytes=64)
-        nc.vector.quantize_mx(out=z_codes[0][:].bitcast(FP8X4), scales=z_plane[0][:], in_=z_rounded[0][:])
+        last_cells = relayed("last_cells", 5, (P, 2, M))
+        nc.vector.tensor_tensor(last_cells[:, 0, :], pages[PAGE_OF[6]][:].indirect(fetch[:]), echo[6][:], ADD)
+        scatter(7)
         for m0 in (0, half_m):
             nc.vector.tensor_tensor(
                 last_cells[:, 1, m0 : m0 + half_m],
-                pages[(FUSED + 1) % PAGES][:].indirect(fetch[:, m0 // 16 : (m0 + half_m) // 16]),
+                pages[PAGE_OF[FUSED + 1]][:].indirect(fetch[:, m0 // 16 : (m0 + half_m) // 16]),
                 echo[FUSED + 1][:, m0 : m0 + half_m],
                 ADD,
             )

from contextlib import ExitStack

import concourse.mybir as mybir
from concourse.masks import make_identity

K, T, S, H, T2, M, N = 1536, 2048, 512, 1024, 1024, 512, 768
FLOPS = 2 * (K * H * S + 2 * H * N * M)

F32 = mybir.dt.float32
BF16 = mybir.dt.bfloat16
I32 = mybir.dt.int32
U32 = mybir.dt.uint32
U16 = mybir.dt.uint16
U8 = mybir.dt.uint8
FP8X4 = mybir.dt.float8_e4m3fn_x4
FP4X4 = mybir.dt.float4_e2m1fn_x4
MULT = mybir.AluOpType.mult
ADD = mybir.AluOpType.add
TANH = mybir.ActivationFunctionType.Tanh
ABS = mybir.ActivationFunctionType.Abs

P = 128
PACK = 4
KP = P * PACK
K_PASSES = K // KP
H_PASSES = H // KP
SLICES = H_PASSES * PACK
N_TILES = N // P
PAGES = 3
PAGE_OF = (0, 1, 2, 1, 0, 2, 1, 2)
FUSED = SLICES - 2
BANKS = 8


def tile_list_beam_slot_features_kernel(
    tc, tab_words, tab_scales, offs, offs2, offs3, w1, b1, gm, wgs, bed, w2_words, w2_scales, gv, w3, out
):
    nc = tc.nc
    with ExitStack() as ctx:
        lists = ctx.enter_context(tc.tile_pool(name="lists", bufs=1))
        keep = ctx.enter_context(tc.tile_pool(name="keep", bufs=1))
        relay = ctx.enter_context(tc.tile_pool(name="relay", bufs=1))
        psum = ctx.enter_context(tc.psum_pool(name="psum", bufs=1))

        pick = lists.tile([P, S // 16], U16, name="pick")
        put = lists.tile([P, S // 16], U16, name="put")
        fetch = lists.tile([P, M // 16], U16, name="fetch")

        def bank(i, name):
            return psum.tile([P, 512], F32, name=name, tag="bank%d" % i)

        def staged(name):
            return keep.tile([P, KP * PACK], BF16, name=name, tag="staged", bufs=3, align_bytes=64)

        def slot(tag, name, shape=(P, S), dtype=F32):
            return keep.tile(list(shape), dtype, name=name, tag=tag, align_bytes=64)

        tab_plane = keep.tile([P, T], U8, name="tab_plane", align_bytes=64)
        nc.vector.memset(tab_plane[:].bitcast(I32), 0)
        for q in range(4):
            nc.scalar.dma_start(
                out=tab_plane[32 * q : 32 * q + 4 * K_PASSES, :].bitcast(I32),
                in_=tab_scales[:, 4 * q : 4 * q + 4, :].bitcast(I32),
            )
        identity = keep.tile([P, P], F32, name="identity")
        make_identity(nc, identity[:])
        w2_plane = keep.tile([P, H_PASSES * N], U8, name="w2_plane", align_bytes=64)
        nc.vector.memset(w2_plane[:].bitcast(I32), 0)

        pages = [keep.tile([P, T2], F32, name="page%d" % i) for i in range(PAGES)]
        for page in pages:
            nc.vector.memset(page[:], 0.0)

        w1_raw = {}

        def load_w1(b, a):
            w1_raw[b, a] = keep.tile([P, PACK, KP], F32, name="w1_raw%d%d" % (b, a), tag="w1_raw", bufs=K_PASSES)
            nc.sync.dma_start(
                out=w1_raw[b, a][:],
                in_=w1[a * KP : (a + 1) * KP, b * KP : (b + 1) * KP].rearrange("(p j) c -> p j c", j=PACK),
            )

        gain = {}
        echo = {}
        gm_rows = gm.rearrange("(b p i) j -> b i p j", p=P, i=PACK)
        bed_rows = bed.rearrange("(b p i) m -> b i p m", p=P, i=PACK)

        def load_gm(s):
            gain[s] = slot("gain%d" % s, "gain%d" % s)
            nc.sync.dma_start(out=gain[s][:], in_=gm_rows[s // PACK, s % PACK])

        def load_bed(s):
            echo[s] = keep.tile([P, M], F32, name="echo%d" % s)
            nc.sync.dma_start(out=echo[s][:], in_=bed_rows[s // PACK, s % PACK])

        w3_raw = {}

        def load_w3(b):
            w3_raw[b] = slot("w3_raw%d" % b, "w3_raw%d" % b, (P, PACK, N))
            nc.sync.dma_start(out=w3_raw[b][:], in_=w3[b * KP : (b + 1) * KP, :].rearrange("(p j) c -> p j c", j=PACK))

        w1_codes = {}
        w1_plane = {}

        def round_w1(copy, rounded, b, a):
            copy(
                out=rounded.rearrange("p (i m j) -> p m j i", i=PACK, j=PACK),
                in_=w1_raw[b, a][:].rearrange("p j (m i) -> p m j i", i=PACK),
            )

        def quantise_w1(copy, b, a, codes_tag):
            rounded = staged("w1_bf%d%d" % (b, a))
            round_w1(copy, rounded[:], b, a)
            codes = slot(codes_tag, "w1_codes%d%d" % (b, a), (P, KP), U32)
            plane = keep.tile([P, KP], U8, name="w1_plane%d%d" % (b, a), align_bytes=64)
            nc.vector.quantize_mx(out=codes[:].bitcast(FP8X4), scales=plane[:], in_=rounded[:])
            w1_codes[b, a], w1_plane[b, a] = codes[:], plane[:]

        def relayed(name, row, shape=(P, M), dtype=F32):
            return relay.tile(list(shape), dtype, name=name, offset=row * M * 4, align_bytes=64)

        def quantise_w1_tail():
            rounded = relayed("w1_bf_tail", 0, (P, 2 * KP * PACK), BF16)
            codes = keep.tile([P, 2 * KP], U32, name="w1_tail_codes", align_bytes=64)
            plane = keep.tile([P, 2 * KP], U8, name="w1_tail_plane", align_bytes=64)
            for a in (1, 2):
                round_w1(nc.scalar.copy, rounded[:, (a - 1) * KP * PACK : a * KP * PACK], 1, a)
                w1_codes[1, a] = codes[:, (a - 1) * KP : a * KP]
                w1_plane[1, a] = plane[:, (a - 1) * KP : a * KP]
            nc.vector.quantize_mx(out=codes[:].bitcast(FP8X4), scales=plane[:], in_=rounded[:])

        squashed = {}

        def first_product(s):
            b, i = divmod(s, PACK)
            acc = bank(s, "h_acc%d" % s)
            cols = slice(i * P, (i + 1) * P)
            for a in range(K_PASSES):
                nc.tensor.matmul_mx(
                    out=acc[:],
                    lhsT=w1_codes[b, a][:, cols].bitcast(FP8X4),
                    lhsT_scale=w1_plane[b, a][:, cols],
                    rhs=picked_words[a][:].bitcast(FP8X4),
                    rhs_scale=picked_plane[4 * a : P, :],
                    start=(a == 0),
                    stop=(a == K_PASSES - 1),
                )
            squashed[s] = slot("squashed%d" % s, "squashed%d" % s)
            nc.scalar.activation(out=squashed[s][:], in_=acc[:], func=TANH, bias=bias[:, s : s + 1])

        weighted = {}

        def weigh(s):
            factor = relayed("factor%d" % s, 0) if s >= PACK else slot("squashed0", "factor%d" % s)
            nc.gpsimd.tensor_tensor(factor[:], gain[s][:], slot_weight[:], MULT)
            weighted[s] = slot("gain%d" % (s % 2), "weighted%d" % s)
            nc.gpsimd.tensor_tensor(weighted[s][:], squashed[s][:], factor[:], MULT)

        def scatter(s):
            nc.vector.tensor_copy(pages[PAGE_OF[s]][:].indirect(put[:]), weighted[s][:])

        turned = {}

        def gather(s, cells):
            nc.vector.tensor_copy(cells, pages[PAGE_OF[s]][:].indirect(fetch[:]))

        def add_echo(s, cells):
            pair, e = divmod(s, 2)
            if e == 0:
                turned[pair] = [bank(h, "turned%d_%d" % (pair, h)) for h in range(2)]
            for mt in range(M // P):
                spot = turned[pair][mt // 2][:, (mt % 2 * 2 + e) * P : (mt % 2 * 2 + e + 1) * P]
                cols = slice(mt * P, (mt + 1) * P)
                nc.tensor.matmul(spot, echo[s][:, cols], identity[:], start=True, stop=False, is_transpose=True)
                nc.tensor.matmul(spot, cells[:, cols], identity[:], start=False, stop=True, is_transpose=True)

        def round_pair(pair, spot_of):
            both = slot("w3_raw1" if pair == 1 else "pairs%d" % pair, "pairs%d" % pair, (P, 2 * M), BF16)
            for h in range(2):
                pairs = both[:, h * M : (h + 1) * M]
                nc.scalar.copy(
                    out=pairs.rearrange("q (mt p e) -> q mt p e", mt=2, e=2),
                    in_=turned[pair][h][:].rearrange("q (mt e p) -> q mt p e", mt=2, e=2),
                )
                for mt in range(2):
                    nc.tensor.transpose(
                        spot_of(2 * h + mt), pairs.bitcast(F32)[:, mt * P : (mt + 1) * P], identity[:]
                    )

        def interleave(copy, rounded, raw):
            copy(
                out=rounded.rearrange("p (c i j) -> p c j i", i=4, j=PACK),
                in_=raw.rearrange("p j (c i) -> p c j i", i=4),
            )

        w3_codes = {}
        w3_plane = [keep.tile([P, N], U8, name="w3_plane%d" % b, align_bytes=64) for b in range(H_PASSES)]

        w3_pieces = [(b, c0, c1) for b in range(H_PASSES) for c0, c1 in ((0, N - 512), (N - 512, N))]
        w3_rounded = {}

        def round_w3():
            for b, c0, c1 in w3_pieces:
                if (b, c0, c1) == w3_pieces[-1]:
                    whole = keep.tile([P, KP * PACK], BF16, name="w3_bf_tail", align_bytes=64)
                else:
                    whole = staged("w3_bf%d_%d" % (b, c0))
                w3_rounded[b, c0] = whole[:, : (c1 - c0) * PACK]
                interleave(nc.scalar.copy, w3_rounded[b, c0], w3_raw[b][:, :, c0:c1])

        def quantise_w3():
            codes = slot("squashed6", "w3_codes", (P, H_PASSES * N), U32)
            for b in range(H_PASSES):
                w3_codes[b] = codes[:, b * N : (b + 1) * N]
            for b, c0, c1 in w3_pieces:
                nc.vector.quantize_mx(
                    out=w3_codes[b][:, c0:c1].bitcast(FP8X4), scales=w3_plane[b][:, c0:c1], in_=w3_rounded[b, c0]
                )

        z_codes = {}
        z_plane = {}
        sums = {}

        def second_pass(n, b):
            cols = slice(n * P, (n + 1) * P)
            if b == 0:
                sums[n] = (bank((2 * n + 4) % BANKS, "y1_%d" % n), bank((2 * n + 5) % BANKS, "y2_%d" % n))
            y1, y2 = sums[n]
            nc.tensor.matmul_mx(
                out=y1[:], lhsT=w2_codes[:, b, 2 * n * P : 2 * (n + 1) * P].bitcast(FP4X4),
                lhsT_scale=w2_plane[:, b * N + n * P : b * N + (n + 1) * P],
                rhs=z_codes[b][:].bitcast(FP8X4), rhs_scale=z_plane[b][:], start=(b == 0), stop=(b == H_PASSES - 1),
            )
            nc.tensor.matmul_mx(
                out=y2[:], lhsT=w3_codes[b][:, cols].bitcast(FP8X4), lhsT_scale=w3_plane[b][:, cols],
                rhs=z_codes[b][:].bitcast(FP8X4), rhs_scale=z_plane[b][:], start=(b == 0), stop=(b == H_PASSES - 1),
            )

        gated = {}
        size = {}

        def leave_banks(n):
            y1, y2 = sums[n]
            size[n] = slot("squashed%d" % (0, 1, 3, 7, 4, 5)[n], "size%d" % n)
            nc.scalar.activation(out=size[n][:], in_=y2[:], func=ABS)
            gated[n] = slot("gain%d" % (n + 2), "gated%d" % n)
            nc.vector.tensor_tensor(gated[n][:], y1[:], gate[n // 3][:, n % 3, :], MULT)

        def finish(n, m0, m1):
            nc.vector.tensor_tensor(gated[n][:, m0:m1], gated[n][:, m0:m1], size[n][:, m0:m1], ADD)
            nc.sync.dma_start(out=out[n * P : (n + 1) * P, m0:m1], in_=gated[n][:, m0:m1])

        nc.sync.dma_start(pick[:], offs)
        nc.sync.dma_start(fetch[:], offs3)
        bias = keep.tile([P, SLICES], F32, name="bias")
        nc.sync.dma_start(out=bias[:].rearrange("p (b i) -> p b i", i=PACK), in_=b1.rearrange("(b p i) -> p b i", p=P, i=PACK))
        nc.sync.dma_start(put[:], offs2)
        for a in range(K_PASSES):
            load_w1(0, a)
        for a in range(K_PASSES):
            quantise_w1(nc.scalar.copy, 0, a, "w1_codes0%d" % a)
        picked_plane = keep.tile([P, S], U8, name="picked_plane", align_bytes=64)
        nc.vector.tensor_copy(picked_plane[:], tab_plane[:].indirect(pick[:]))
        picked_words = []
        for a in range(K_PASSES):
            table = keep.tile([P, T], U32, name="table%d" % a, align_bytes=64)
            nc.sync.dma_start(out=table[:].bitcast(I32), in_=tab_words[a].rearrange("p t i -> p (t i)").bitcast(I32))
            words = keep.tile([P, S], U32, name="picked_words%d" % a, align_bytes=64)
            nc.vector.tensor_copy(words[:], table[:].indirect(pick[:]))
            picked_words.append(words)
        slot_weight = keep.tile([P, S], F32, name="slot_weight")
        nc.sync.dma_start(out=slot_weight[:], in_=wgs)
        load_gm(0)
        load_gm(1)
        load_gm(2)
        load_gm(3)
        for a in range(K_PASSES):
            load_w1(1, a)
        for s in range(PACK, SLICES):
            load_gm(s)
        for b in range(H_PASSES):
            load_bed(2 * b)
            load_bed(2 * b + 1)
            load_w3(b)
        load_bed(4)
        load_bed(5)
        w2_codes = keep.tile([P, H_PASSES, 2 * N], U8, name="w2_codes", align_bytes=64)
        nc.sync.dma_start(out=w2_codes[:].bitcast(I32), in_=w2_words.bitcast(I32).rearrange("b p c -> p b c"))
        for q in range(4):
            nc.sync.dma_start(
                out=w2_plane[32 * q : 32 * q + 4, :].bitcast(I32).rearrange("r (b c) -> r b c", b=H_PASSES),
                in_=w2_scales[:, 4 * q : 4 * q + 4, :].bitcast(I32).rearrange("b r c -> r b c"),
            )
        load_bed(6)
        load_bed(7)
        gate = []
        for half in range(2):
            rows = keep.tile([P, 3, M], F32, name="gate%d" % half)
            nc.sync.dma_start(out=rows[:], in_=gv[half * 3 * P : (half + 1) * 3 * P, :].rearrange("(n p) m -> p n m", p=P))
            gate.append(rows)

        half_m = M // 2
        z_rounded = [
            relayed("z_bf0", 4, (P, M * PACK), BF16),
            keep.tile([P, M * PACK], BF16, name="z_bf1", align_bytes=64),
        ]
        z_words = [z_rounded[b][:].bitcast(F32).rearrange("p (m u) -> p m u", u=2) for b in range(H_PASSES)]
        nc.vector.tensor_tensor(gain[0][:], gain[0][:], slot_weight[:], MULT)
        factor1 = slot("factor1", "factor1")
        nc.vector.tensor_tensor(factor1[:], gain[1][:], slot_weight[:], MULT)
        for s in range(PACK):
            first_product(s)
        nc.vector.tensor_tensor(pages[PAGE_OF[0]][:].indirect(put[:]), squashed[0][:], gain[0][:], MULT)
        weighted[1] = slot("gain1", "weighted1")
        nc.vector.tensor_tensor(weighted[1][:], squashed[1][:], factor1[:], MULT)
        scatter(1)
        weigh(2)
        cells0 = slot("factor1", "cells0")
        gather(0, cells0[:])
        add_echo(0, cells0[:])
        scatter(2)
        weigh(3)
        quantise_w1(nc.scalar.copy, 1, 0, "squashed2")
        quantise_w1_tail()
        for s in range(PACK, SLICES):
            first_product(s)
        cells1 = relayed("cells1", 1)
        gather(1, cells1[:])
        add_echo(1, cells1[:])
        back = [bank(2 + h, "back0_%d" % h) for h in range(2)]
        round_pair(0, lambda mt: back[mt // 2][:, mt % 2 * P : (mt % 2 + 1) * P])
        cells2 = relayed("cells2", 2)
        gather(2, cells2[:])
        add_echo(2, cells2[:])
        weigh(4)
        scatter(3)
        weigh(5)
        scatter(4)
        weigh(6)
        cells3 = slot("squashed4", "cells3")
        gather(3, cells3[:])
        add_echo(3, cells3[:])
        scatter(5)
        weigh(7)
        cells4 = slot("squashed5", "cells4")
        gather(4, cells4[:])
        round_w3()
        round_pair(1, lambda mt: back[mt // 2][:, half_m + mt % 2 * P : half_m + (mt % 2 + 1) * P])
        for h in range(2):
            nc.scalar.copy(
                out=z_words[0][:, h * half_m : (h + 1) * half_m, :],
                in_=back[h][:].rearrange("p (u m) -> p m u", u=2),
            )
        add_echo(4, cells4[:])
        scatter(6)
        quantise_w3()
        z_codes[0] = relayed("z_codes0", 0, (P, M), U32)
        z_plane[0] = keep.tile([P, M], U8, name="z_plane0", align_bytes=64)
        nc.vector.quantize_mx(out=z_codes[0][:].bitcast(FP8X4), scales=z_plane[0][:], in_=z_rounded[0][:])
        cells5 = relayed("cells5", 4)
        gather(5, cells5[:])
        add_echo(5, cells5[:])
        back1 = bank(2, "back1")
        round_pair(2, lambda mt: back1[:, mt * P : (mt + 1) * P])
        nc.scalar.copy(out=z_words[1][:, :, 0], in_=back1[:])

        last_cells = relayed("last_cells", 5, (P, 2, M))
        nc.vector.tensor_tensor(last_cells[:, 0, :], pages[PAGE_OF[6]][:].indirect(fetch[:]), echo[6][:], ADD)
        scatter(7)
        for m0 in (0, half_m):
            nc.vector.tensor_tensor(
                last_cells[:, 1, m0 : m0 + half_m],
                pages[PAGE_OF[FUSED + 1]][:].indirect(fetch[:, m0 // 16 : (m0 + half_m) // 16]),
                echo[FUSED + 1][:, m0 : m0 + half_m],
                ADD,
            )
        for n in range(BANKS // 2):
            second_pass(n, 0)
        z_codes[1] = keep.tile([P, M], U32, name="z_codes1", align_bytes=64)
        z_plane[1] = keep.tile([P, M], U8, name="z_plane1", align_bytes=64)
        upper = z_rounded[1][:].rearrange("p (c i j) -> p c j i", i=4, j=PACK)[:, :, 2:4, :]
        for m0 in (0, half_m):
            nc.vector.tensor_copy(
                out=upper[:, m0 // 4 : (m0 + half_m) // 4],
                in_=last_cells[:, :, m0 : m0 + half_m].rearrange("p e (c i) -> p c e i", i=4),
            )
        for m0 in (0, half_m):
            nc.vector.quantize_mx(
                out=z_codes[1][:, m0 : m0 + half_m].bitcast(FP8X4), scales=z_plane[1][:, m0 : m0 + half_m],
                in_=z_rounded[1][:, m0 * PACK : (m0 + half_m) * PACK],
            )
        for n in range(N_TILES):
            if n >= BANKS // 2:
                second_pass(n, 0)
            second_pass(n, 1)
            leave_banks(n)
            if n > 0:
                finish(n - 1, 0, M)
        finish(N_TILES - 1, 0, half_m)
        finish(N_TILES - 1, half_m, M)
